import numpy as np
import ml_dtypes


def mxq(x, axis, fmt="e4m3"):
    dtype, down = {"e4m3": (ml_dtypes.float8_e4m3fn, 7), "e5m2": (ml_dtypes.float8_e5m2, 14)}[fmt]
    v = np.moveaxis(np.asarray(x, np.float32).astype(ml_dtypes.bfloat16).astype(np.float64), axis, -1)
    blocks = v.reshape(v.shape[:-1] + (-1, 32))
    amax = np.abs(blocks).max(-1, keepdims=True)
    byte = np.maximum(np.where(amax > 0, np.frexp(amax)[1] - 1 + 127, 0) - down, 1)
    scale = np.exp2(byte - 127.0)
    codes = (blocks / scale).astype(np.float32).astype(dtype).astype(np.float64)
    return np.moveaxis((codes * scale).reshape(v.shape), -1, axis)


WIDE = False


def mx_kscale(k):
    if not WIDE:
        return np.ones(k)
    levels = np.array([10, -10, 5, -5, 0])
    if k % 512:
        return np.exp2(np.random.permutation(np.resize(levels, k // 32))).repeat(32)
    a = np.empty((k // 512, 16))
    for p in range(k // 512):
        a[p, :8] = np.random.permutation(np.resize(levels, 8))
        for g in range(8):
            far = levels[np.abs(levels - a[p, g]) >= 10]
            a[p, g + 8] = far[np.random.randint(len(far))]
    return np.exp2(a.ravel()).repeat(32)


def f64(x):
    return np.asarray(x).astype(np.float64)


def striped(idx):
    return np.tile(np.asarray(idx).reshape(-1, 16).T, (8, 1)).astype(np.uint16)


def unstriped(offs):
    return offs[:16].T.reshape(-1).astype(np.int64)


def sigmoid(v):
    return 1.0 / (1.0 + np.exp(-v))


D, T, I, Q, E, U, M = 512, 2048, 512, 512, 512, 1024, 1024


def setup_inputs():
    n = np.random.standard_normal
    idx = np.random.permutation(T)[:I]
    idx2 = np.random.permutation(U)[:I]
    idx3 = np.random.permutation(M)[:I]
    fd = mx_kscale(D)
    fq = mx_kscale(Q)
    return {
        "query": (n((D, Q)) * 0.9 / np.sqrt(D) * fd[:, None]).astype(np.float32),
        "keys": (n((D, T)) / fd[:, None]).astype(np.float32),
        "notes": (n((D, U)) / fd[:, None]).astype(np.float32),
        "qs": (np.random.uniform(0.5, 2.0, (Q, 1)) * fq[:, None]).astype(np.float32),
        "msgs": (n((Q, E)) * 1 / np.sqrt(Q) / fq[:, None]).astype(np.float32),
        "old": (n((E, M)) * 1.0).astype(np.float32),
        "fade": (np.random.uniform(0.3, 0.9, (1, M))).astype(np.float32),
        "offs": striped(idx),
        "offs2": striped(idx2),
        "offs3": striped(idx3),
    }


def reference(query, keys, notes, qs, msgs, old, fade, offs, offs2, offs3):
    idx = unstriped(offs)
    idx2 = unstriped(offs2)
    idx3 = unstriped(offs3)
    zk = np.abs(f64(keys)[:, idx] - f64(notes)[:, idx2])
    queryq = mxq(f64(query), 0, "e4m3")
    zkq = mxq(zk, 0, "e4m3")
    s = queryq.T @ zkq
    w = sigmoid(s)
    wq = w * f64(qs)
    msgsq = mxq(f64(msgs), 0, "e4m3")
    wqq = mxq(wq, 0, "e4m3")
    dl = msgsq.T @ wqq
    df = np.zeros((E, M))
    df[:, idx3] = dl
    y = f64(old) * f64(fade) + df
    return y

@@ -1,0 +1,191 @@
+from contextlib import ExitStack
+
+import concourse.mybir as mybir
+from concourse.masks import make_identity
+
+D, T, I, Q, E, U, M = 512, 2048, 512, 512, 512, 1024, 1024
+FLOPS = 2 * D * Q * I + 2 * Q * E * I
+
+F32 = mybir.dt.float32
+BF16 = mybir.dt.bfloat16
+U32 = mybir.dt.uint32
+U16 = mybir.dt.uint16
+U8 = mybir.dt.uint8
+FP8X4 = mybir.dt.float8_e4m3fn_x4
+ACT = mybir.ActivationFunctionType
+ALU = mybir.AluOpType
+
+P = 128
+PACK = 4
+CH = 128
+NCH = I // CH
+HALF = 512
+
+
+def tile_attend_keyapart_delivered_lean_kernel(tc, query, keys, notes, qs, msgs, old, fade, offs, offs2, offs3, out):
+    nc = tc.nc
+    with ExitStack() as ctx:
+        sb = ctx.enter_context(tc.tile_pool(name="sb", bufs=1))
+        ps = ctx.enter_context(tc.psum_pool(name="ps", bufs=1))
+
+        def cols(lst, a, b):
+            return lst[:, a // 16 : b // 16]
+
+        o1 = sb.tile([P, I // 16], U16, name="o1")
+        o2 = sb.tile([P, I // 16], U16, name="o2")
+        o3 = sb.tile([P, I // 16], U16, name="o3")
+        kt = [sb.tile([P, T], F32, name=f"k{t}") for t in range(PACK)]
+        nt = [sb.tile([P, U], F32, name=f"n{t}") for t in range(PACK)]
+        q_raw = sb.tile([P, PACK, Q], F32, name="q_raw")
+        m_raw = sb.tile([P, PACK, E], F32, name="m_raw")
+        old_t = [sb.tile([P, M], F32, name=f"old{e}") for e in range(4)]
+        qs_sb = sb.tile([P, PACK], F32, name="qs_sb")
+        fade_sb = sb.tile([P, 2, PACK], F32, name="fade_sb")
+
+        keys_v = keys.rearrange("(p t) n -> t p n", t=PACK)
+        notes_v = notes.rearrange("(p t) n -> t p n", t=PACK)
+        nc.sync.dma_start(nt[0][:], notes_v[0])
+        nc.sync.dma_start(o2[:], offs2)
+        nc.sync.dma_start(o1[:], offs)
+        nc.sync.dma_start(kt[0][:], keys_v[0])
+        nc.sync.dma_start(nt[1][:], notes_v[1])
+        nc.sync.dma_start(kt[1][:], keys_v[1])
+        nc.sync.dma_start(fade_sb[:], fade.rearrange("o (h p j) -> p (o h) j", h=2, j=PACK))
+        nc.sync.dma_start(qs_sb[:], qs.rearrange("(p t) o -> p (t o)", t=PACK))
+        nc.sync.dma_start(o3[:], offs3)
+        for t in (2, 3):
+            nc.sync.dma_start(nt[t][:], notes_v[t])
+            nc.sync.dma_start(kt[t][:], keys_v[t])
+        nc.sync.dma_start(q_raw[:], query.rearrange("(p j) q -> p j q", j=PACK))
+        nc.sync.dma_start(m_raw[:], msgs.rearrange("(p j) e -> p j e", j=PACK))
+        for e in range(4):
+            nc.sync.dma_start(old_t[e][:], old[e * P : (e + 1) * P, :])
+
+        ident = sb.tile([P, P], F32, name="ident")
+        make_identity(nc, ident[:])
+        win = [sb.tile([P, M], F32, name=f"win{e}") for e in range(4)]
+        for e in range(4):
+            nc.gpsimd.memset(win[e][:], 0.0)
+
+        fade_ps = [ps.tile([P, PACK, P], F32, name=f"fade_ps{h}") for h in range(2)]
+        for h in range(2):
+            for j in range(PACK):
+                nc.tensor.transpose(fade_ps[h][:, j, :], fade_sb[:, h, j : j + 1].to_broadcast([P, P]), ident[:])
+
+        gn = [sb.tile([P, I], F32, name=f"gn{t}") for t in range(PACK)]
+        diff01 = sb.tile([P, 2, I], F32, name="diff01")
+        diff23 = [sb.tile([P, 2, CH], F32, name=f"diff23_{c}") for c in range(NCH)]
+        zk_bf = [sb.tile([P, CH, PACK], BF16, name=f"zk_bf{c}", align_bytes=64) for c in range(NCH)]
+        zk_w = [sb.tile([P, CH], U32, name=f"zk_w{c}", align_bytes=64) for c in range(NCH)]
+        zk_s = [sb.tile([P, CH], U8, name=f"zk_s{c}", align_bytes=64) for c in range(NCH)]
+        for t in range(2):
+            nc.scalar.activation(gn[t][:], nt[t][:].indirect(o2[:]), ACT.Copy)
+            nc.vector.tensor_tensor(diff01[:, t, :], kt[t][:].indirect(o1[:]), gn[t][:], ALU.subtract)
+        nc.scalar.activation(gn[2][:], nt[2][:].indirect(o2[:]), ACT.Copy)
+        for c in range(NCH):
+            nc.vector.tensor_tensor(
+                diff23[c][:, 0, :], kt[2][:].indirect(cols(o1, c * CH, (c + 1) * CH)), gn[2][:, c * CH : (c + 1) * CH], ALU.subtract
+            )
+        for c in range(NCH):
+            nc.scalar.activation(
+                zk_bf[c][:, :, 0:2], diff01[:, :, c * CH : (c + 1) * CH].rearrange("p t i -> p i t"), ACT.Abs
+            )
+        nc.scalar.activation(gn[3][:], nt[3][:].indirect(o2[:]), ACT.Copy)
+        for c in range(NCH):
+            nc.vector.tensor_tensor(
+                diff23[c][:, 1, :], kt[3][:].indirect(cols(o1, c * CH, (c + 1) * CH)), gn[3][:, c * CH : (c + 1) * CH], ALU.subtract
+            )
+            nc.scalar.activation(zk_bf[c][:, :, 2:4], diff23[c][:].rearrange("p t i -> p i t"), ACT.Abs)
+        for c in range(NCH):
+            nc.vector.quantize_mx(zk_w[c][:].bitcast(FP8X4), zk_s[c][:], zk_bf[c][:].rearrange("p i t -> p (i t)"))
+
+        q_bf = sb.tile([P, Q * PACK], BF16, name="q_bf", align_bytes=64)
+        q_w = sb.tile([P, Q], U32, name="q_w", align_bytes=64)
+        q_s = sb.tile([P, Q], U8, name="q_s", align_bytes=64)
+        q_dst = q_bf[:].rearrange("p (t m j) -> p m j t", t=PACK, j=PACK)
+        q_src = q_raw[:].rearrange("p j (m t) -> p m j t", t=PACK)
+        MS = 84
+        nc.vector.tensor_copy(q_dst[:, 0:MS], q_src[:, 0:MS])
+        nc.scalar.copy(q_dst[:, MS:P], q_src[:, MS:P])
+        nc.vector.quantize_mx(q_w[:].bitcast(FP8X4), q_s[:], q_bf[:])
+
+        m_bf = sb.tile([P, E * PACK], BF16, name="m_bf", align_bytes=64)
+        m_w = sb.tile([P, E], U32, name="m_w", align_bytes=64)
+        m_s = sb.tile([P, E], U8, name="m_s", align_bytes=64)
+
+        dl = sb.tile([P, 4, I], F32, name="dl")
+        w = [sb.tile([P, CH, PACK], F32, name=f"w{c}") for c in range(NCH)]
+        wq_bf = [sb.tile([P, CH, PACK], BF16, name=f"wq_bf{c}", align_bytes=64) for c in range(NCH)]
+        wq_w = [sb.tile([P, CH], U32, name=f"wq_w{c}", align_bytes=64) for c in range(NCH)]
+        wq_s = [sb.tile([P, CH], U8, name=f"wq_s{c}", align_bytes=64) for c in range(NCH)]
+        for c in range(NCH):
+            s_ps = ps.tile([P, PACK, CH], F32, name="s_ps", tag="s_ps", bufs=3)
+            for t in range(PACK):
+                nc.tensor.matmul_mx(
+                    s_ps[:, t, :],
+                    lhsT=q_w[:, t * P : (t + 1) * P].bitcast(FP8X4),
+                    lhsT_scale=q_s[:, t * P : (t + 1) * P],
+                    rhs=zk_w[c][:].bitcast(FP8X4),
+                    rhs_scale=zk_s[c][:],
+                    start=True,
+                    stop=True,
+                )
+            nc.scalar.activation(w[c][:], s_ps[:].rearrange("p t i -> p i t"), ACT.Sigmoid)
+        m_dst = m_bf[:].rearrange("p (c i t) -> p c t i", i=4, t=PACK)
+        m_src = m_raw[:].rearrange("p t (c i) -> p c t i", i=4)
+        nc.vector.tensor_copy(m_dst, m_src)
+        nc.vector.quantize_mx(m_w[:].bitcast(FP8X4), m_s[:], m_bf[:])
+        def weigh(c):
+            nc.vector.tensor_tensor(wq_bf[c][:], w[c][:], qs_sb[:].unsqueeze(1).to_broadcast([P, CH, PACK]), ALU.mult)
+
+        weigh(0)
+        for c in range(NCH):
+            if c + 1 < NCH:
+                weigh(c + 1)
+            nc.vector.quantize_mx(wq_w[c][:].bitcast(FP8X4), wq_s[c][:], wq_bf[c][:].rearrange("p i t -> p (i t)"))
+            d_ps = ps.tile([P, 4, CH], F32, name="d_ps", tag="d_ps", bufs=3)
+            for e in range(4):
+                nc.tensor.matmul_mx(
+                    d_ps[:, e, :],
+                    lhsT=m_w[:, e * P : (e + 1) * P].bitcast(FP8X4),
+                    lhsT_scale=m_s[:, e * P : (e + 1) * P],
+                    rhs=wq_w[c][:].bitcast(FP8X4),
+                    rhs_scale=wq_s[c][:],
+                    start=True,
+                    stop=True,
+                )
+            nc.scalar.copy(dl[:, :, c * CH : (c + 1) * CH], d_ps[:])
+
+        def faded(e):
+            for h in range(2):
+                blk = old_t[e][:, h * HALF : (h + 1) * HALF].rearrange("p (n j) -> p n j", j=PACK)
+                nc.vector.tensor_tensor(blk, blk, fade_ps[h][:].rearrange("p j n -> p n j"), ALU.mult)
+
+        def scat_s(e, a, b):
+            nc.scalar.activation(win[e][:].indirect(cols(o3, a, b)), dl[:, e, a:b], ACT.Copy)
+
+        def scat_v(e, a, b):
+            nc.vector.tensor_copy(win[e][:].indirect(cols(o3, a, b)), dl[:, e, a:b])
+
+        def finish(e):
+            for h in range(2):
+                blk = old_t[e][:, h * HALF : (h + 1) * HALF]
+                nc.vector.tensor_tensor(blk, blk, win[e][:, h * HALF : (h + 1) * HALF], ALU.add)
+                nc.sync.dma_start(out[e * P : (e + 1) * P, h * HALF : (h + 1) * HALF], blk)
+
+        scat_v(0, 0, 256)
+        scat_s(1, 0, 256)
+        scat_v(0, 256, 512)
+        scat_s(1, 256, 512)
+        faded(0)
+        finish(0)
+        scat_s(2, 0, 256)
+        scat_s(2, 256, 512)
+        faded(1)
+        finish(1)
+        scat_s(3, 0, 256)
+        scat_s(3, 256, 512)
+        faded(2)
+        finish(2)
+        faded(3)
+        finish(3)

@@ -37,8 +37,9 @@ def tile_attend_keyapart_delivered_lean_kernel(tc, query, keys, notes, qs, msgs,
         kt = [sb.tile([P, T], F32, name=f"k{t}") for t in range(PACK)]
         nt = [sb.tile([P, U], F32, name=f"n{t}") for t in range(PACK)]
         q_raw = sb.tile([P, PACK, Q], F32, name="q_raw")
-        m_raw = sb.tile([P, PACK, E], F32, name="m_raw")
-        old_t = [sb.tile([P, M], F32, name=f"old{e}") for e in range(4)]
+        m_raw = [sb.tile([P, 2, E], F32, name=f"m_raw{u}") for u in range(2)]
+        old01 = sb.tile([P, 2 * M], F32, name="old01")
+        old_t = [old01[:, 0:M], old01[:, M : 2 * M]] + [sb.tile([P, M], F32, name=f"old{e}")[:] for e in (2, 3)]
         qs_sb = sb.tile([P, PACK], F32, name="qs_sb")
         fade_sb = sb.tile([P, 2, PACK], F32, name="fade_sb")
 
@@ -51,15 +52,17 @@ def tile_attend_keyapart_delivered_lean_kernel(tc, query, keys, notes, qs, msgs,
         nc.sync.dma_start(nt[1][:], notes_v[1])
         nc.sync.dma_start(kt[1][:], keys_v[1])
         nc.sync.dma_start(fade_sb[:], fade.rearrange("o (h p j) -> p (o h) j", h=2, j=PACK))
-        nc.sync.dma_start(qs_sb[:], qs.rearrange("(p t) o -> p (t o)", t=PACK))
-        nc.sync.dma_start(o3[:], offs3)
         for t in (2, 3):
             nc.sync.dma_start(nt[t][:], notes_v[t])
             nc.sync.dma_start(kt[t][:], keys_v[t])
         nc.sync.dma_start(q_raw[:], query.rearrange("(p j) q -> p j q", j=PACK))
-        nc.sync.dma_start(m_raw[:], msgs.rearrange("(p j) e -> p j e", j=PACK))
-        for e in range(4):
-            nc.sync.dma_start(old_t[e][:], old[e * P : (e + 1) * P, :])
+        for u in range(2):
+            nc.sync.dma_start(m_raw[u][:], msgs.rearrange("(p j) e -> p j e", j=PACK)[:, 2 * u : 2 * u + 2, :])
+        nc.sync.dma_start(qs_sb[:], qs.rearrange("(p t) o -> p (t o)", t=PACK))
+        nc.sync.dma_start(o3[:], offs3)
+        for e in (2, 3):
+            nc.sync.dma_start(old_t[e], old[e * P : (e + 1) * P, :])
+        nc.sync.dma_start(old01[:].rearrange("p (e m) -> p e m", e=2), old[0 : 2 * P, :].rearrange("(e p) m -> p e m", e=2))
 
         ident = sb.tile([P, P], F32, name="ident")
         make_identity(nc, ident[:])
@@ -72,10 +75,17 @@ def tile_attend_keyapart_delivered_lean_kernel(tc, query, keys, notes, qs, msgs,
             for j in range(PACK):
                 nc.tensor.transpose(fade_ps[h][:, j, :], fade_sb[:, h, j : j + 1].to_broadcast([P, P]), ident[:])
 
+        fade_row = sb.tile([P, M], F32, name="fade_row")
+        for h in range(2):
+            nc.scalar.copy(
+                fade_row[:, h * HALF : (h + 1) * HALF].rearrange("p (n j) -> p n j", j=PACK), fade_ps[h][:].rearrange("p j n -> p n j")
+            )
+
         gn = [sb.tile([P, I], F32, name=f"gn{t}") for t in range(PACK)]
         diff01 = sb.tile([P, 2, I], F32, name="diff01")
         diff23 = [sb.tile([P, 2, CH], F32, name=f"diff23_{c}") for c in range(NCH)]
-        zk_bf = [sb.tile([P, CH, PACK], BF16, name=f"zk_bf{c}", align_bytes=64) for c in range(NCH)]
+        zk_bf = [sb.tile([P, CH, PACK], BF16, name=f"zk_bf{c}", align_bytes=64) for c in range(NCH - 1)]
+        zk_bf.append(sb.tile([P, CH, PACK], BF16, name="zk_bf_last", tag="stage", align_bytes=64))
         zk_w = [sb.tile([P, CH], U32, name=f"zk_w{c}", align_bytes=64) for c in range(NCH)]
         zk_s = [sb.tile([P, CH], U8, name=f"zk_s{c}", align_bytes=64) for c in range(NCH)]
         for t in range(2):
@@ -99,7 +109,7 @@ def tile_attend_keyapart_delivered_lean_kernel(tc, query, keys, notes, qs, msgs,
         for c in range(NCH):
             nc.vector.quantize_mx(zk_w[c][:].bitcast(FP8X4), zk_s[c][:], zk_bf[c][:].rearrange("p i t -> p (i t)"))
 
-        q_bf = sb.tile([P, Q * PACK], BF16, name="q_bf", align_bytes=64)
+        q_bf = sb.tile([P, Q * PACK], BF16, name="q_bf", tag="stage", align_bytes=64)
         q_w = sb.tile([P, Q], U32, name="q_w", align_bytes=64)
         q_s = sb.tile([P, Q], U8, name="q_s", align_bytes=64)
         q_dst = q_bf[:].rearrange("p (t m j) -> p m j t", t=PACK, j=PACK)
@@ -109,13 +119,20 @@ def tile_attend_keyapart_delivered_lean_kernel(tc, query, keys, notes, qs, msgs,
         nc.scalar.copy(q_dst[:, MS:P], q_src[:, MS:P])
         nc.vector.quantize_mx(q_w[:].bitcast(FP8X4), q_s[:], q_bf[:])
 
-        m_bf = sb.tile([P, E * PACK], BF16, name="m_bf", align_bytes=64)
+        m_bf = sb.tile([P, E * PACK], BF16, name="m_bf", tag="stage", align_bytes=64)
         m_w = sb.tile([P, E], U32, name="m_w", align_bytes=64)
         m_s = sb.tile([P, E], U8, name="m_s", align_bytes=64)
 
+        m_dst = m_bf[:].rearrange("p (c i t) -> p c t i", i=4, t=PACK)
+        for u in range(2):
+            nc.vector.tensor_copy(m_dst[:, :, 2 * u : 2 * u + 2, :], m_raw[u][:].rearrange("p t (c i) -> p c t i", i=4))
+        nc.vector.quantize_mx(m_w[:].bitcast(FP8X4), m_s[:], m_bf[:])
+
         dl = sb.tile([P, 4, I], F32, name="dl")
-        w = [sb.tile([P, CH, PACK], F32, name=f"w{c}") for c in range(NCH)]
-        wq_bf = [sb.tile([P, CH, PACK], BF16, name=f"wq_bf{c}", align_bytes=64) for c in range(NCH)]
+        w_all = sb.tile([P, I * PACK], F32, name="w_all")
+        w = [w_all[:, c * CH * PACK : (c + 1) * CH * PACK].rearrange("p (i t) -> p i t", t=PACK) for c in range(NCH)]
+        wq_bf = [sb.tile([P, CH, PACK], BF16, name=f"wq_bf{c}", align_bytes=64) for c in range(NCH - 1)]
+        wq_bf.append(sb.tile([P, CH, PACK], BF16, name="wq_bf_last", tag="stage", align_bytes=64))
         wq_w = [sb.tile([P, CH], U32, name=f"wq_w{c}", align_bytes=64) for c in range(NCH)]
         wq_s = [sb.tile([P, CH], U8, name=f"wq_s{c}", align_bytes=64) for c in range(NCH)]
         for c in range(NCH):
@@ -130,13 +147,9 @@ def tile_attend_keyapart_delivered_lean_kernel(tc, query, keys, notes, qs, msgs,
                     start=True,
                     stop=True,
                 )
-            nc.scalar.activation(w[c][:], s_ps[:].rearrange("p t i -> p i t"), ACT.Sigmoid)
-        m_dst = m_bf[:].rearrange("p (c i t) -> p c t i", i=4, t=PACK)
-        m_src = m_raw[:].rearrange("p t (c i) -> p c t i", i=4)
-        nc.vector.tensor_copy(m_dst, m_src)
-        nc.vector.quantize_mx(m_w[:].bitcast(FP8X4), m_s[:], m_bf[:])
+            nc.scalar.activation(w[c], s_ps[:].rearrange("p t i -> p i t"), ACT.Sigmoid)
         def weigh(c):
-            nc.vector.tensor_tensor(wq_bf[c][:], w[c][:], qs_sb[:].unsqueeze(1).to_broadcast([P, CH, PACK]), ALU.mult)
+            nc.vector.tensor_tensor(wq_bf[c][:], w[c], qs_sb[:].unsqueeze(1).to_broadcast([P, CH, PACK]), ALU.mult)
 
         weigh(0)
         for c in range(NCH):
@@ -156,10 +169,16 @@ def tile_attend_keyapart_delivered_lean_kernel(tc, query, keys, notes, qs, msgs,
                 )
             nc.scalar.copy(dl[:, :, c * CH : (c + 1) * CH], d_ps[:])
 
-        def faded(e):
-            for h in range(2):
-                blk = old_t[e][:, h * HALF : (h + 1) * HALF].rearrange("p (n j) -> p n j", j=PACK)
-                nc.vector.tensor_tensor(blk, blk, fade_ps[h][:].rearrange("p j n -> p n j"), ALU.mult)
+        halves = [old_t[e][:, h * HALF : (h + 1) * HALF] for e in range(4) for h in range(2)]
+        res2 = sb.tile([P, M], F32, name="res2", tag="stage", align_bytes=64)
+        res = halves[0:4] + [res2[:, 0:HALF], res2[:, HALF:M], halves[0], halves[1]]
+        out0 = sb.tile([P, M], F32, name="out0")
+        total = [out0[:, 0:HALF], out0[:, HALF:M], res[2], halves[6], halves[7], res[3], res[4], res[5]]
+
+        def faded(k):
+            src = halves[k].rearrange("p (n j) -> p n j", j=PACK)
+            dst = res[k].rearrange("p (n j) -> p n j", j=PACK)
+            nc.vector.tensor_tensor(dst, src, fade_ps[k % 2][:].rearrange("p j n -> p n j"), ALU.mult)
 
         def scat_s(e, a, b):
             nc.scalar.activation(win[e][:].indirect(cols(o3, a, b)), dl[:, e, a:b], ACT.Copy)
@@ -167,25 +186,27 @@ def tile_attend_keyapart_delivered_lean_kernel(tc, query, keys, notes, qs, msgs,
         def scat_v(e, a, b):
             nc.vector.tensor_copy(win[e][:].indirect(cols(o3, a, b)), dl[:, e, a:b])
 
-        def finish(e):
-            for h in range(2):
-                blk = old_t[e][:, h * HALF : (h + 1) * HALF]
-                nc.vector.tensor_tensor(blk, blk, win[e][:, h * HALF : (h + 1) * HALF], ALU.add)
-                nc.sync.dma_start(out[e * P : (e + 1) * P, h * HALF : (h + 1) * HALF], blk)
+        def finish(k, eng, a=0, b=HALF):
+            e, c0 = k // 2, (k % 2) * HALF
+            blk = total[k][:, a:b]
+            eng.tensor_tensor(blk, res[k][:, a:b], win[e][:, c0 + a : c0 + b], ALU.add)
+            nc.sync.dma_start(out[e * P : (e + 1) * P, c0 + a : c0 + b], blk)
 
+        for k in range(4):
+            nc.gpsimd.tensor_tensor(res[k], halves[k], fade_row[:, (k % 2) * HALF : (k % 2 + 1) * HALF], ALU.mult)
         scat_v(0, 0, 256)
-        scat_s(1, 0, 256)
         scat_v(0, 256, 512)
-        scat_s(1, 256, 512)
-        faded(0)
-        finish(0)
-        scat_s(2, 0, 256)
-        scat_s(2, 256, 512)
-        faded(1)
-        finish(1)
-        scat_s(3, 0, 256)
-        scat_s(3, 256, 512)
-        faded(2)
-        finish(2)
-        faded(3)
-        finish(3)
+        scat_s(1, 320, 512)
+        scat_v(1, 0, 320)
+        scat_s(2, 384, 512)
+        scat_s(3, 384, 512)
+        scat_s(2, 0, 384)
+        scat_s(3, 0, 384)
+        for k in range(3):
+            finish(k, nc.gpsimd)
+        for k in range(4, 8):
+            faded(k)
+        for k in range(3, 7):
+            finish(k, nc.vector)
+        finish(7, nc.vector, 0, 256)
+        finish(7, nc.vector, 256, 512)

@@ -38,8 +38,7 @@ def tile_attend_keyapart_delivered_lean_kernel(tc, query, keys, notes, qs, msgs,
         nt = [sb.tile([P, U], F32, name=f"n{t}") for t in range(PACK)]
         q_raw = sb.tile([P, PACK, Q], F32, name="q_raw")
         m_raw = [sb.tile([P, 2, E], F32, name=f"m_raw{u}") for u in range(2)]
-        old01 = sb.tile([P, 2 * M], F32, name="old01")
-        old_t = [old01[:, 0:M], old01[:, M : 2 * M]] + [sb.tile([P, M], F32, name=f"old{e}")[:] for e in (2, 3)]
+        old_t = [sb.tile([P, M], F32, name=f"old{e}")[:] for e in range(4)]
         qs_sb = sb.tile([P, PACK], F32, name="qs_sb")
         fade_sb = sb.tile([P, 2, PACK], F32, name="fade_sb")
 
@@ -51,18 +50,17 @@ def tile_attend_keyapart_delivered_lean_kernel(tc, query, keys, notes, qs, msgs,
         nc.sync.dma_start(kt[0][:], keys_v[0])
         nc.sync.dma_start(nt[1][:], notes_v[1])
         nc.sync.dma_start(kt[1][:], keys_v[1])
-        nc.sync.dma_start(fade_sb[:], fade.rearrange("o (h p j) -> p (o h) j", h=2, j=PACK))
+        nc.scalar.dma_start(fade_sb[:], fade.rearrange("o (h p j) -> p (o h) j", h=2, j=PACK))
+        nc.scalar.dma_start(qs_sb[:], qs.rearrange("(p t) o -> p (t o)", t=PACK))
         for t in (2, 3):
             nc.sync.dma_start(nt[t][:], notes_v[t])
             nc.sync.dma_start(kt[t][:], keys_v[t])
         nc.sync.dma_start(q_raw[:], query.rearrange("(p j) q -> p j q", j=PACK))
         for u in range(2):
             nc.sync.dma_start(m_raw[u][:], msgs.rearrange("(p j) e -> p j e", j=PACK)[:, 2 * u : 2 * u + 2, :])
-        nc.sync.dma_start(qs_sb[:], qs.rearrange("(p t) o -> p (t o)", t=PACK))
         nc.sync.dma_start(o3[:], offs3)
-        for e in (2, 3):
+        for e in range(4):
             nc.sync.dma_start(old_t[e], old[e * P : (e + 1) * P, :])
-        nc.sync.dma_start(old01[:].rearrange("p (e m) -> p e m", e=2), old[0 : 2 * P, :].rearrange("(e p) m -> p e m", e=2))
 
         ident = sb.tile([P, P], F32, name="ident")
         make_identity(nc, ident[:])
@@ -170,8 +168,9 @@ def tile_attend_keyapart_delivered_lean_kernel(tc, query, keys, notes, qs, msgs,
             nc.scalar.copy(dl[:, :, c * CH : (c + 1) * CH], d_ps[:])
 
         halves = [old_t[e][:, h * HALF : (h + 1) * HALF] for e in range(4) for h in range(2)]
-        res2 = sb.tile([P, M], F32, name="res2", tag="stage", align_bytes=64)
-        res = halves[0:4] + [res2[:, 0:HALF], res2[:, HALF:M], halves[0], halves[1]]
+        faded_t = sb.tile([P, 3 * M], F32, name="faded_t", tag="stage", align_bytes=64)
+        res = [faded_t[:, k * HALF : (k + 1) * HALF] for k in range(6)]
+        res = res + res[0:2]
         out0 = sb.tile([P, M], F32, name="out0")
         total = [out0[:, 0:HALF], out0[:, HALF:M], res[2], halves[6], halves[7], res[3], res[4], res[5]]
 

from contextlib import ExitStack

import concourse.mybir as mybir
from concourse.masks import make_identity

D, T, I, Q, E, U, M = 512, 2048, 512, 512, 512, 1024, 1024
FLOPS = 2 * D * Q * I + 2 * Q * E * I

F32 = mybir.dt.float32
BF16 = mybir.dt.bfloat16
U32 = mybir.dt.uint32
U16 = mybir.dt.uint16
U8 = mybir.dt.uint8
FP8X4 = mybir.dt.float8_e4m3fn_x4
ACT = mybir.ActivationFunctionType
ALU = mybir.AluOpType

P = 128
PACK = 4
CH = 128
NCH = I // CH
HALF = 512


def tile_attend_keyapart_delivered_lean_kernel(tc, query, keys, notes, qs, msgs, old, fade, offs, offs2, offs3, out):
    nc = tc.nc
    with ExitStack() as ctx:
        sb = ctx.enter_context(tc.tile_pool(name="sb", bufs=1))
        ps = ctx.enter_context(tc.psum_pool(name="ps", bufs=1))

        def cols(lst, a, b):
            return lst[:, a // 16 : b // 16]

        o1 = sb.tile([P, I // 16], U16, name="o1")
        o2 = sb.tile([P, I // 16], U16, name="o2")
        o3 = sb.tile([P, I // 16], U16, name="o3")
        kt = [sb.tile([P, T], F32, name=f"k{t}") for t in range(PACK)]
        nt = [sb.tile([P, U], F32, name=f"n{t}") for t in range(PACK)]
        q_raw = sb.tile([P, PACK, Q], F32, name="q_raw")
        m_raw = [sb.tile([P, 2, E], F32, name=f"m_raw{u}") for u in range(2)]
        old_t = [sb.tile([P, M], F32, name=f"old{e}")[:] for e in range(4)]
        qs_sb = sb.tile([P, PACK], F32, name="qs_sb")
        fade_sb = sb.tile([P, 2, PACK], F32, name="fade_sb")

        keys_v = keys.rearrange("(p t) n -> t p n", t=PACK)
        notes_v = notes.rearrange("(p t) n -> t p n", t=PACK)
        nc.sync.dma_start(nt[0][:], notes_v[0])
        nc.sync.dma_start(o2[:], offs2)
        nc.sync.dma_start(o1[:], offs)
        nc.sync.dma_start(kt[0][:], keys_v[0])
        nc.sync.dma_start(nt[1][:], notes_v[1])
        nc.sync.dma_start(kt[1][:], keys_v[1])
        nc.scalar.dma_start(fade_sb[:], fade.rearrange("o (h p j) -> p (o h) j", h=2, j=PACK))
        nc.scalar.dma_start(qs_sb[:], qs.rearrange("(p t) o -> p (t o)", t=PACK))
        for t in (2, 3):
            nc.sync.dma_start(nt[t][:], notes_v[t])
            nc.sync.dma_start(kt[t][:], keys_v[t])
        nc.sync.dma_start(q_raw[:], query.rearrange("(p j) q -> p j q", j=PACK))
        for u in range(2):
            nc.sync.dma_start(m_raw[u][:], msgs.rearrange("(p j) e -> p j e", j=PACK)[:, 2 * u : 2 * u + 2, :])
        nc.sync.dma_start(o3[:], offs3)
        for e in range(4):
            nc.sync.dma_start(old_t[e], old[e * P : (e + 1) * P, :])

        ident = sb.tile([P, P], F32, name="ident")
        make_identity(nc, ident[:])
        win = [sb.tile([P, M], F32, name=f"win{e}") for e in range(4)]
        for e in range(4):
            nc.gpsimd.memset(win[e][:], 0.0)

        fade_ps = [ps.tile([P, PACK, P], F32, name=f"fade_ps{h}") for h in range(2)]
        for h in range(2):
            for j in range(PACK):
                nc.tensor.transpose(fade_ps[h][:, j, :], fade_sb[:, h, j : j + 1].to_broadcast([P, P]), ident[:])

        fade_row = sb.tile([P, M], F32, name="fade_row")
        for h in range(2):
            nc.scalar.copy(
                fade_row[:, h * HALF : (h + 1) * HALF].rearrange("p (n j) -> p n j", j=PACK), fade_ps[h][:].rearrange("p j n -> p n j")
            )

        gn = [sb.tile([P, I], F32, name=f"gn{t}") for t in range(PACK)]
        diff01 = sb.tile([P, 2, I], F32, name="diff01")
        diff23 = [sb.tile([P, 2, CH], F32, name=f"diff23_{c}") for c in range(NCH)]
        zk_bf = [sb.tile([P, CH, PACK], BF16, name=f"zk_bf{c}", align_bytes=64) for c in range(NCH - 1)]
        zk_bf.append(sb.tile([P, CH, PACK], BF16, name="zk_bf_last", tag="stage", align_bytes=64))
        zk_w = [sb.tile([P, CH], U32, name=f"zk_w{c}", align_bytes=64) for c in range(NCH)]
        zk_s = [sb.tile([P, CH], U8, name=f"zk_s{c}", align_bytes=64) for c in range(NCH)]
        for t in range(2):
            nc.scalar.activation(gn[t][:], nt[t][:].indirect(o2[:]), ACT.Copy)
            nc.vector.tensor_tensor(diff01[:, t, :], kt[t][:].indirect(o1[:]), gn[t][:], ALU.subtract)
        nc.scalar.activation(gn[2][:], nt[2][:].indirect(o2[:]), ACT.Copy)
        for c in range(NCH):
            nc.vector.tensor_tensor(
                diff23[c][:, 0, :], kt[2][:].indirect(cols(o1, c * CH, (c + 1) * CH)), gn[2][:, c * CH : (c + 1) * CH], ALU.subtract
            )
        for c in range(NCH):
            nc.scalar.activation(
                zk_bf[c][:, :, 0:2], diff01[:, :, c * CH : (c + 1) * CH].rearrange("p t i -> p i t"), ACT.Abs
            )
        nc.scalar.activation(gn[3][:], nt[3][:].indirect(o2[:]), ACT.Copy)
        for c in range(NCH):
            nc.vector.tensor_tensor(
                diff23[c][:, 1, :], kt[3][:].indirect(cols(o1, c * CH, (c + 1) * CH)), gn[3][:, c * CH : (c + 1) * CH], ALU.subtract
            )
            nc.scalar.activation(zk_bf[c][:, :, 2:4], diff23[c][:].rearrange("p t i -> p i t"), ACT.Abs)
        for c in range(NCH):
            nc.vector.quantize_mx(zk_w[c][:].bitcast(FP8X4), zk_s[c][:], zk_bf[c][:].rearrange("p i t -> p (i t)"))

        q_bf = sb.tile([P, Q * PACK], BF16, name="q_bf", tag="stage", align_bytes=64)
        q_w = sb.tile([P, Q], U32, name="q_w", align_bytes=64)
        q_s = sb.tile([P, Q], U8, name="q_s", align_bytes=64)
        q_dst = q_bf[:].rearrange("p (t m j) -> p m j t", t=PACK, j=PACK)
        q_src = q_raw[:].rearrange("p j (m t) -> p m j t", t=PACK)
        MS = 84
        nc.vector.tensor_copy(q_dst[:, 0:MS], q_src[:, 0:MS])
        nc.scalar.copy(q_dst[:, MS:P], q_src[:, MS:P])
        nc.vector.quantize_mx(q_w[:].bitcast(FP8X4), q_s[:], q_bf[:])

        m_bf = sb.tile([P, E * PACK], BF16, name="m_bf", tag="stage", align_bytes=64)
        m_w = sb.tile([P, E], U32, name="m_w", align_bytes=64)
        m_s = sb.tile([P, E], U8, name="m_s", align_bytes=64)

        m_dst = m_bf[:].rearrange("p (c i t) -> p c t i", i=4, t=PACK)
        for u in range(2):
            nc.vector.tensor_copy(m_dst[:, :, 2 * u : 2 * u + 2, :], m_raw[u][:].rearrange("p t (c i) -> p c t i", i=4))
        nc.vector.quantize_mx(m_w[:].bitcast(FP8X4), m_s[:], m_bf[:])

        dl = sb.tile([P, 4, I], F32, name="dl")
        w_all = sb.tile([P, I * PACK], F32, name="w_all")
        w = [w_all[:, c * CH * PACK : (c + 1) * CH * PACK].rearrange("p (i t) -> p i t", t=PACK) for c in range(NCH)]
        wq_bf = [sb.tile([P, CH, PACK], BF16, name=f"wq_bf{c}", align_bytes=64) for c in range(NCH - 1)]
        wq_bf.append(sb.tile([P, CH, PACK], BF16, name="wq_bf_last", tag="stage", align_bytes=64))
        wq_w = [sb.tile([P, CH], U32, name=f"wq_w{c}", align_bytes=64) for c in range(NCH)]
        wq_s = [sb.tile([P, CH], U8, name=f"wq_s{c}", align_bytes=64) for c in range(NCH)]
        for c in range(NCH):
            s_ps = ps.tile([P, PACK, CH], F32, name="s_ps", tag="s_ps", bufs=3)
            for t in range(PACK):
                nc.tensor.matmul_mx(
                    s_ps[:, t, :],
                    lhsT=q_w[:, t * P : (t + 1) * P].bitcast(FP8X4),
                    lhsT_scale=q_s[:, t * P : (t + 1) * P],
                    rhs=zk_w[c][:].bitcast(FP8X4),
                    rhs_scale=zk_s[c][:],
                    start=True,
                    stop=True,
                )
            nc.scalar.activation(w[c], s_ps[:].rearrange("p t i -> p i t"), ACT.Sigmoid)
        def weigh(c):
            nc.vector.tensor_tensor(wq_bf[c][:], w[c], qs_sb[:].unsqueeze(1).to_broadcast([P, CH, PACK]), ALU.mult)

        weigh(0)
        for c in range(NCH):
            if c + 1 < NCH:
                weigh(c + 1)
            nc.vector.quantize_mx(wq_w[c][:].bitcast(FP8X4), wq_s[c][:], wq_bf[c][:].rearrange("p i t -> p (i t)"))
            d_ps = ps.tile([P, 4, CH], F32, name="d_ps", tag="d_ps", bufs=3)
            for e in range(4):
                nc.tensor.matmul_mx(
                    d_ps[:, e, :],
                    lhsT=m_w[:, e * P : (e + 1) * P].bitcast(FP8X4),
                    lhsT_scale=m_s[:, e * P : (e + 1) * P],
                    rhs=wq_w[c][:].bitcast(FP8X4),
                    rhs_scale=wq_s[c][:],
                    start=True,
                    stop=True,
                )
            nc.scalar.copy(dl[:, :, c * CH : (c + 1) * CH], d_ps[:])

        halves = [old_t[e][:, h * HALF : (h + 1) * HALF] for e in range(4) for h in range(2)]
        faded_t = sb.tile([P, 3 * M], F32, name="faded_t", tag="stage", align_bytes=64)
        res = [faded_t[:, k * HALF : (k + 1) * HALF] for k in range(6)]
        res = res + res[0:2]
        out0 = sb.tile([P, M], F32, name="out0")
        total = [out0[:, 0:HALF], out0[:, HALF:M], res[2], halves[6], halves[7], res[3], res[4], res[5]]

        def faded(k):
            src = halves[k].rearrange("p (n j) -> p n j", j=PACK)
            dst = res[k].rearrange("p (n j) -> p n j", j=PACK)
            nc.vector.tensor_tensor(dst, src, fade_ps[k % 2][:].rearrange("p j n -> p n j"), ALU.mult)

        def scat_s(e, a, b):
            nc.scalar.activation(win[e][:].indirect(cols(o3, a, b)), dl[:, e, a:b], ACT.Copy)

        def scat_v(e, a, b):
            nc.vector.tensor_copy(win[e][:].indirect(cols(o3, a, b)), dl[:, e, a:b])

        def finish(k, eng, a=0, b=HALF):
            e, c0 = k // 2, (k % 2) * HALF
            blk = total[k][:, a:b]
            eng.tensor_tensor(blk, res[k][:, a:b], win[e][:, c0 + a : c0 + b], ALU.add)
            nc.sync.dma_start(out[e * P : (e + 1) * P, c0 + a : c0 + b], blk)

        for k in range(4):
            nc.gpsimd.tensor_tensor(res[k], halves[k], fade_row[:, (k % 2) * HALF : (k % 2 + 1) * HALF], ALU.mult)
        scat_v(0, 0, 256)
        scat_v(0, 256, 512)
        scat_s(1, 320, 512)
        scat_v(1, 0, 320)
        scat_s(2, 384, 512)
        scat_s(3, 384, 512)
        scat_s(2, 0, 384)
        scat_s(3, 0, 384)
        for k in range(3):
            finish(k, nc.gpsimd)
        for k in range(4, 8):
            faded(k)
        for k in range(3, 7):
            finish(k, nc.vector)
        finish(7, nc.vector, 0, 256)
        finish(7, nc.vector, 256, 512)
